import numpy as np
import ml_dtypes


def mxq(x, axis, fmt="e4m3"):
    dtype, down = {"e4m3": (ml_dtypes.float8_e4m3fn, 7), "e5m2": (ml_dtypes.float8_e5m2, 14)}[fmt]
    v = np.moveaxis(np.asarray(x, np.float32).astype(ml_dtypes.bfloat16).astype(np.float64), axis, -1)
    blocks = v.reshape(v.shape[:-1] + (-1, 32))
    amax = np.abs(blocks).max(-1, keepdims=True)
    byte = np.maximum(np.where(amax > 0, np.frexp(amax)[1] - 1 + 127, 0) - down, 1)
    scale = np.exp2(byte - 127.0)
    codes = (blocks / scale).astype(np.float32).astype(dtype).astype(np.float64)
    return np.moveaxis((codes * scale).reshape(v.shape), -1, axis)


WIDE = False


def mx_kscale(k):
    if not WIDE:
        return np.ones(k)
    levels = np.array([10, -10, 5, -5, 0])
    if k % 512:
        return np.exp2(np.random.permutation(np.resize(levels, k // 32))).repeat(32)
    a = np.empty((k // 512, 16))
    for p in range(k // 512):
        a[p, :8] = np.random.permutation(np.resize(levels, 8))
        for g in range(8):
            far = levels[np.abs(levels - a[p, g]) >= 10]
            a[p, g + 8] = far[np.random.randint(len(far))]
    return np.exp2(a.ravel()).repeat(32)


def f64(x):
    return np.asarray(x).astype(np.float64)


def striped(idx):
    return np.tile(idx.reshape(-1, 16).T, (8, 1)).astype(np.uint16)


def unstriped(offs):
    return offs[:16].T.reshape(-1).astype(np.int64)


def pack_weight(w):
    k, n = w.shape
    w = f64(np.asarray(w, np.float32).astype(ml_dtypes.bfloat16)).reshape(k // 32, 32, n)
    amax = np.abs(w).max(1)
    byte = np.clip(np.where(amax > 0, np.frexp(amax)[1] - 1 + 127 - 7, 1), 1, 254)
    scaled = (w * np.exp2(127.0 - byte)[:, None, :]).reshape(k, n).astype(np.float32)
    words = np.ascontiguousarray(scaled.reshape(k // 512, 128, 4, n).transpose(0, 1, 3, 2)).astype(ml_dtypes.float8_e4m3fn).view(np.uint8)
    return words, np.ascontiguousarray(byte.astype(np.uint8).reshape(k // 512, 16, n))


def unpack_weight(words, scales):
    g, p, n, _ = words.shape
    vals = np.ascontiguousarray(words).view(ml_dtypes.float8_e4m3fn).astype(np.float64) * np.repeat(np.exp2(scales.astype(np.float64) - 127.0), 8, axis=1)[..., None]
    return vals.transpose(0, 1, 3, 2).reshape(g * 512, n)


def sigmoid(v):
    return 1.0 / (1.0 + np.exp(-np.maximum(v, -700.0)))


K, T, S, V = 512, 1024, 512, 256
P = 2 ** 7


def setup_inputs():
    n = np.random.standard_normal
    s = mx_kscale(K)[:, None]
    packed_xT = pack_weight(n((K, T)) * s)
    return {
        "x_words": packed_xT[0],
        "x_scales": packed_xT[1],
        "hT": (n((K, V)) / np.sqrt(K) / s).astype(np.float32),
        "gT": (n((K, V)) / np.sqrt(K) / s).astype(np.float32),
        "good": (np.tile(np.where(np.random.uniform(size=S) < 0.5, 1.0, -1.0), (P, 1))).astype(np.float32),
        "lam": (np.tile(np.random.uniform(0.5, 1.5, S), (P, 1))).astype(np.float32),
        "offs": striped(np.random.permutation(T)[:S]),
    }


def reference(x_words, x_scales, hT, gT, good, lam, offs):
    hTq = mxq(f64(hT), 0, "e4m3")
    xq = unpack_weight(x_words, x_scales)[:, unstriped(offs)]
    y = hTq.T @ xq
    ea = np.exp(y)
    sa = np.log(ea.sum(axis=1, keepdims=True))
    la = y - sa
    gTq = mxq(f64(gT), 0, "e4m3")
    z = gTq.T @ xq
    eb = np.exp(z)
    sb = np.log(eb.sum(axis=1, keepdims=True))
    lb = z - sb
    rwd = la - lb
    ad = np.abs(rwd)
    zref = ad.mean(axis=1, keepdims=True)
    val = sigmoid(1.5 * (f64(good)[:1] * (rwd - (0.3 * zref))))
    return ((f64(lam)[:1] * f64(good)[:1]) * val) * (-1.0 * val + 1.0)

@@ -1,0 +1,182 @@
+from contextlib import ExitStack
+
+import concourse.mybir as mybir
+
+K, T, S, V = 512, 1024, 512, 256
+FLOPS = 2 * 2 * K * V * S
+
+F32 = mybir.dt.float32
+BF16 = mybir.dt.bfloat16
+I32 = mybir.dt.int32
+U32 = mybir.dt.uint32
+U16 = mybir.dt.uint16
+U8 = mybir.dt.uint8
+FP8X4 = mybir.dt.float8_e4m3fn_x4
+ALU = mybir.AluOpType
+ACT = mybir.ActivationFunctionType
+
+P = 128
+PACK = 4
+TILES = V // P
+HALF_BETA = 0.75
+ZREF_SHARE = 0.3
+LOG_PER_BIT = 355.0 / 512.0 / 2.0**23
+DEGREE = 20
+STEPS = DEGREE + 2
+
+
+def tile_picked_yhkto_grad_p_kernel(tc, x_words, x_scales, hT, gT, good, lam, offs, out):
+    nc = tc.nc
+    with ExitStack() as ctx:
+        keep = ctx.enter_context(tc.tile_pool(name="keep", bufs=1))
+        psum = ctx.enter_context(tc.psum_pool(name="psum", bufs=1))
+
+        offsets = keep.tile([P, S // 16], U16, name="offsets")
+        table_scales = keep.tile([P, T], U8, name="table_scales", align_bytes=64)
+        table_words = keep.tile([P, T], I32, name="table_words", align_bytes=64)
+        h_raw = keep.tile([P, PACK, V], F32, name="h_raw", tag="reused")
+        g_raw = keep.tile([P, PACK, V], F32, name="g_raw")
+
+        nc.vector.memset(table_scales[:].bitcast(I32), 0)
+        nc.sync.dma_start(offsets[:], offs)
+        nc.sync.dma_start(h_raw[:], hT.rearrange("(p j) w -> p j w", j=PACK))
+        for q in range(4):
+            nc.sync.dma_start(
+                table_scales[32 * q : 32 * q + 4, :].bitcast(I32),
+                x_scales[0, 4 * q : 4 * q + 4, :].bitcast(I32),
+            )
+        nc.sync.dma_start(table_words[:], x_words[0].rearrange("p n t -> p (n t)").bitcast(I32))
+        nc.sync.dma_start(g_raw[:], gT.rearrange("(p j) w -> p j w", j=PACK))
+
+        orders = keep.tile([P, TILES, DEGREE], F32, name="orders")
+        inverse_orders = keep.tile([P, TILES, DEGREE], F32, name="inverse_orders")
+        factors = keep.tile([P, TILES, STEPS], F32, name="factors")
+        terms = keep.tile([P, TILES, STEPS], F32, name="terms")
+        nc.gpsimd.iota(
+            orders[:], [[0, TILES], [-1, DEGREE]], base=DEGREE, channel_multiplier=0,
+            allow_small_or_imprecise_dtypes=True,
+        )
+        nc.vector.reciprocal(inverse_orders[:], orders[:])
+        nc.scalar.activation(terms[:, :, 0:DEGREE], inverse_orders[:], ACT.Copy, scale=-1.0)
+        nc.vector.memset(factors[:, :, DEGREE + 1], HALF_BETA)
+
+        picked_scales = keep.tile([P, S], U8, name="picked_scales", align_bytes=64)
+        picked_words = keep.tile([P, S], U32, name="picked_words", align_bytes=64)
+        nc.vector.tensor_copy(picked_scales[:], table_scales[:].indirect(offsets[:]))
+
+        def interleave(engine, raw, t, name):
+            grouped = keep.tile([P, P, PACK], BF16, name=name, align_bytes=64)
+            dst = grouped[:].rearrange("p (c i) j -> p c j i", i=4)
+            src = raw[:, :, t * P : (t + 1) * P].rearrange("p j (c i) -> p c j i", i=4)
+            if engine is nc.scalar:
+                nc.scalar.copy(dst, src)
+            else:
+                nc.vector.tensor_copy(dst, src)
+            return grouped
+
+        def quantize(grouped, name):
+            codes = keep.tile([P, P], U32, name=name + "_codes", align_bytes=64)
+            scales = keep.tile([P, P], U8, name=name + "_scales", align_bytes=64)
+            nc.vector.quantize_mx(
+                out=codes[:].bitcast(FP8X4),
+                scales=scales[:],
+                in_=grouped[:].rearrange("p w j -> p (w j)"),
+            )
+            return codes, scales
+
+        def product(operand, name):
+            codes, scales = operand
+            bank = psum.tile([P, S], F32, name=name)
+            nc.tensor.matmul_mx(
+                out=bank[:],
+                lhsT=codes[:].bitcast(FP8X4),
+                lhsT_scale=scales[:],
+                rhs=picked_words[:].bitcast(FP8X4),
+                rhs_scale=picked_scales[:],
+                start=True,
+                stop=True,
+            )
+            return bank
+
+        h_bf = [interleave(nc.scalar, h_raw, t, "h_bf%d" % t) for t in range(TILES)]
+        labels = keep.tile([P, 2, S], F32, name="labels", tag="reused")
+        lam_sb, good_sb = labels[:, 0, :], labels[:, 1, :]
+        nc.sync.dma_start(lam_sb, lam)
+        nc.sync.dma_start(good_sb, good)
+        h_mx = [quantize(h_bf[t], "h%d" % t) for t in range(TILES)]
+        nc.vector.tensor_copy(picked_words[:], table_words[:].bitcast(U32).indirect(offsets[:]))
+        g_bf = [interleave(nc.vector if t == 0 else nc.scalar, g_raw, t, "g_bf%d" % t) for t in range(TILES)]
+        g_mx = [quantize(g_bf[t], "g%d" % t) for t in range(TILES)]
+
+        weight = keep.tile([P, S], F32, name="weight")
+        mins = keep.tile([P, TILES, 2], F32, name="mins")
+        sums = keep.tile([P, TILES, 4], F32, name="sums")
+        small = keep.tile([P, TILES, 4], F32, name="small")
+        guess = keep.tile([P, TILES], F32, name="guess")
+        scanned = keep.tile([P, TILES, STEPS], F32, name="scanned")
+        discard = keep.tile([P, S], F32, name="discard")
+
+        diffs = []
+        for t in range(TILES):
+            neg = []
+            for side, operand in enumerate((h_mx[t], g_mx[t])):
+                bank = product(operand, "bank%d%d" % (t, side))
+                minus = keep.tile([P, S], F32, name="minus%d%d" % (t, side))
+                nc.vector.tensor_scalar(
+                    minus[:], bank[:], -1.0, None, ALU.mult, ALU.min, accum_out=mins[:, t, side : side + 1]
+                )
+                nc.scalar.activation(
+                    discard[:], minus[:], ACT.Exp, bias=mins[:, t, side : side + 1], scale=-1.0,
+                    accum_out=sums[:, t, side : side + 1],
+                )
+                neg.append(minus)
+                if side == 0:
+                    nc.vector.tensor_scalar(
+                        small[:, t, 2:3], sums[:, t, 0:1].bitcast(I32), LOG_PER_BIT, None, ALU.mult
+                    )
+                    nc.vector.reciprocal(small[:, t, 0:1], sums[:, t, 0:1])
+            nc.vector.tensor_scalar(
+                terms[:, t, DEGREE + 1 : DEGREE + 2], mins[:, t, 0:1], mins[:, t, 1:2], HALF_BETA,
+                ALU.subtract, ALU.mult,
+            )
+            diff = keep.tile([P, S], F32, name="diff%d" % t)
+            nc.vector.tensor_tensor(diff[:], neg[1][:], neg[0][:], ALU.subtract)
+            diffs.append(diff)
+
+            nc.scalar.activation(
+                guess[:, t : t + 1], sums[:, t, 1:2].bitcast(U32), ACT.Exp,
+                bias=small[:, t, 2:3], scale=-LOG_PER_BIT,
+            )
+            nc.vector.tensor_scalar(
+                small[:, t, 3:4], sums[:, t, 1:2], small[:, t, 0:1], -1.0, ALU.mult, ALU.mult
+            )
+            nc.vector.tensor_scalar(
+                terms[:, t, DEGREE : DEGREE + 1], sums[:, t, 1:2].bitcast(I32), LOG_PER_BIT, small[:, t, 2:3],
+                ALU.mult, ALU.subtract,
+            )
+            nc.vector.tensor_scalar(
+                factors[:, t, 0 : DEGREE + 1], guess[:, t : t + 1].to_broadcast([P, DEGREE + 1]),
+                small[:, t, 3:4], 1.0, ALU.mult, ALU.add,
+            )
+            nc.vector.tensor_tensor_scan(
+                scanned[:, t, :], factors[:, t, :], terms[:, t, :], 0.0, ALU.mult, ALU.add
+            )
+
+        nc.vector.scalar_tensor_tensor(weight[:], lam_sb, -1.0, good_sb, ALU.mult, ALU.mult)
+
+        for t in range(TILES):
+            shift = scanned[:, t, STEPS - 1 : STEPS]
+            nc.scalar.activation(
+                discard[:], diffs[t][:], ACT.Abs, bias=shift, scale=HALF_BETA, accum_out=sums[:, t, 2:3]
+            )
+            nc.vector.tensor_scalar(
+                small[:, t, 1:2], sums[:, t, 2:3], -ZREF_SHARE / S, shift, ALU.mult, ALU.add
+            )
+        for t in range(TILES):
+            tanh = keep.tile([P, S], F32, name="tanh%d" % t)
+            square = keep.tile([P, S], F32, name="square%d" % t)
+            result = keep.tile([P, S], F32, name="result%d" % t)
+            nc.scalar.activation(tanh[:], diffs[t][:], ACT.Tanh, bias=small[:, t, 1:2], scale=HALF_BETA)
+            nc.scalar.activation(square[:], tanh[:], ACT.Square, scale=0.5)
+            nc.vector.scalar_tensor_tensor(result[:], square[:], 0.25, weight[:], ALU.subtract, ALU.mult)
+            nc.sync.dma_start(out[t * P : (t + 1) * P, :], result[:])

@@ -22,7 +22,8 @@ HALF_BETA = 0.75
 ZREF_SHARE = 0.3
 LOG_PER_BIT = 355.0 / 512.0 / 2.0**23
 DEGREE = 20
-STEPS = DEGREE + 2
+STEPS = DEGREE + 3
+HALF = S // 2
 
 
 def tile_picked_yhkto_grad_p_kernel(tc, x_words, x_scales, hT, gT, good, lam, offs, out):
@@ -32,20 +33,20 @@ def tile_picked_yhkto_grad_p_kernel(tc, x_words, x_scales, hT, gT, good, lam, of
         psum = ctx.enter_context(tc.psum_pool(name="psum", bufs=1))
 
         offsets = keep.tile([P, S // 16], U16, name="offsets")
-        table_scales = keep.tile([P, T], U8, name="table_scales", align_bytes=64)
+        table_scales = keep.tile([P, T], U8, name="table_scales", tag="scales_then_words", align_bytes=64)
         table_words = keep.tile([P, T], I32, name="table_words", align_bytes=64)
         h_raw = keep.tile([P, PACK, V], F32, name="h_raw", tag="reused")
         g_raw = keep.tile([P, PACK, V], F32, name="g_raw")
 
         nc.vector.memset(table_scales[:].bitcast(I32), 0)
         nc.sync.dma_start(offsets[:], offs)
-        nc.sync.dma_start(h_raw[:], hT.rearrange("(p j) w -> p j w", j=PACK))
         for q in range(4):
-            nc.sync.dma_start(
+            nc.scalar.dma_start(
                 table_scales[32 * q : 32 * q + 4, :].bitcast(I32),
                 x_scales[0, 4 * q : 4 * q + 4, :].bitcast(I32),
             )
         nc.sync.dma_start(table_words[:], x_words[0].rearrange("p n t -> p (n t)").bitcast(I32))
+        nc.sync.dma_start(h_raw[:], hT.rearrange("(p j) w -> p j w", j=PACK))
         nc.sync.dma_start(g_raw[:], gT.rearrange("(p j) w -> p j w", j=PACK))
 
         orders = keep.tile([P, TILES, DEGREE], F32, name="orders")
@@ -59,10 +60,13 @@ def tile_picked_yhkto_grad_p_kernel(tc, x_words, x_scales, hT, gT, good, lam, of
         nc.vector.reciprocal(inverse_orders[:], orders[:])
         nc.scalar.activation(terms[:, :, 0:DEGREE], inverse_orders[:], ACT.Copy, scale=-1.0)
         nc.vector.memset(factors[:, :, DEGREE + 1], HALF_BETA)
+        nc.vector.tensor_scalar(factors[:, :, DEGREE + 2], orders[:, :, DEGREE - 1], ZREF_SHARE / S, None, ALU.mult)
+        nc.vector.memset(terms[:, :, DEGREE + 2], 0.0)
 
         picked_scales = keep.tile([P, S], U8, name="picked_scales", align_bytes=64)
-        picked_words = keep.tile([P, S], U32, name="picked_words", align_bytes=64)
         nc.vector.tensor_copy(picked_scales[:], table_scales[:].indirect(offsets[:]))
+        picked_words = keep.tile([P, S], U32, name="picked_words", tag="scales_then_words", align_bytes=64)
+        nc.vector.tensor_copy(picked_words[:], table_words[:].bitcast(U32).indirect(offsets[:]))
 
         def interleave(engine, raw, t, name):
             grouped = keep.tile([P, P, PACK], BF16, name=name, align_bytes=64)
@@ -98,85 +102,107 @@ def tile_picked_yhkto_grad_p_kernel(tc, x_words, x_scales, hT, gT, good, lam, of
             )
             return bank
 
-        h_bf = [interleave(nc.scalar, h_raw, t, "h_bf%d" % t) for t in range(TILES)]
+        engines = (nc.vector, nc.scalar)
+        h_bf = [interleave(engines[t], h_raw, t, "h_bf%d" % t) for t in range(TILES)]
         labels = keep.tile([P, 2, S], F32, name="labels", tag="reused")
         lam_sb, good_sb = labels[:, 0, :], labels[:, 1, :]
         nc.sync.dma_start(lam_sb, lam)
         nc.sync.dma_start(good_sb, good)
         h_mx = [quantize(h_bf[t], "h%d" % t) for t in range(TILES)]
-        nc.vector.tensor_copy(picked_words[:], table_words[:].bitcast(U32).indirect(offsets[:]))
-        g_bf = [interleave(nc.vector if t == 0 else nc.scalar, g_raw, t, "g_bf%d" % t) for t in range(TILES)]
+        g_bf = [interleave(engines[t], g_raw, t, "g_bf%d" % t) for t in range(TILES)]
         g_mx = [quantize(g_bf[t], "g%d" % t) for t in range(TILES)]
 
         weight = keep.tile([P, S], F32, name="weight")
         mins = keep.tile([P, TILES, 2], F32, name="mins")
-        sums = keep.tile([P, TILES, 4], F32, name="sums")
-        small = keep.tile([P, TILES, 4], F32, name="small")
-        guess = keep.tile([P, TILES], F32, name="guess")
+        sums = keep.tile([P, TILES, 3], F32, name="sums")
+        small = keep.tile([P, TILES, 2], F32, name="small")
+        guess = keep.tile([P, TILES, 2], F32, name="guess")
         scanned = keep.tile([P, TILES, STEPS], F32, name="scanned")
-        discard = keep.tile([P, S], F32, name="discard")
 
-        diffs = []
-        for t in range(TILES):
-            neg = []
-            for side, operand in enumerate((h_mx[t], g_mx[t])):
-                bank = product(operand, "bank%d%d" % (t, side))
-                minus = keep.tile([P, S], F32, name="minus%d%d" % (t, side))
-                nc.vector.tensor_scalar(
-                    minus[:], bank[:], -1.0, None, ALU.mult, ALU.min, accum_out=mins[:, t, side : side + 1]
-                )
-                nc.scalar.activation(
-                    discard[:], minus[:], ACT.Exp, bias=mins[:, t, side : side + 1], scale=-1.0,
-                    accum_out=sums[:, t, side : side + 1],
-                )
-                neg.append(minus)
-                if side == 0:
-                    nc.vector.tensor_scalar(
-                        small[:, t, 2:3], sums[:, t, 0:1].bitcast(I32), LOG_PER_BIT, None, ALU.mult
-                    )
-                    nc.vector.reciprocal(small[:, t, 0:1], sums[:, t, 0:1])
+        minus = {}
+
+        def softmax_sum(t, side, operand):
+            bank = product(operand, "bank%d%d" % (t, side))
+            minus[t, side] = keep.tile([P, S], F32, name="minus%d%d" % (t, side))
+            exps = keep.tile([P, S], F32, name="exps%d%d" % (t, side))
+            nc.vector.tensor_scalar(
+                minus[t, side][:], bank[:], -1.0, None, ALU.mult, ALU.min, accum_out=mins[:, t, side : side + 1]
+            )
+            nc.scalar.activation(
+                exps[:], minus[t, side][:], ACT.Exp, bias=mins[:, t, side : side + 1], scale=-1.0,
+                accum_out=sums[:, t, side : side + 1],
+            )
+
+        def first_guess(t):
+            nc.scalar.activation(
+                guess[:, t, 0:1], sums[:, t, 0:1].bitcast(U32), ACT.Copy, scale=LOG_PER_BIT
+            )
+
+        def second_guess(t):
+            nc.scalar.activation(
+                guess[:, t, 1:2], sums[:, t, 1:2].bitcast(U32), ACT.Exp,
+                bias=guess[:, t, 0:1], scale=-LOG_PER_BIT,
+            )
+
+        def log_ratio(t):
+            nc.vector.reciprocal(small[:, t, 0:1], sums[:, t, 0:1])
             nc.vector.tensor_scalar(
                 terms[:, t, DEGREE + 1 : DEGREE + 2], mins[:, t, 0:1], mins[:, t, 1:2], HALF_BETA,
                 ALU.subtract, ALU.mult,
             )
-            diff = keep.tile([P, S], F32, name="diff%d" % t)
-            nc.vector.tensor_tensor(diff[:], neg[1][:], neg[0][:], ALU.subtract)
-            diffs.append(diff)
-
-            nc.scalar.activation(
-                guess[:, t : t + 1], sums[:, t, 1:2].bitcast(U32), ACT.Exp,
-                bias=small[:, t, 2:3], scale=-LOG_PER_BIT,
+            nc.vector.tensor_scalar(
+                small[:, t, 1:2], sums[:, t, 1:2], small[:, t, 0:1], -1.0, ALU.mult, ALU.mult
             )
             nc.vector.tensor_scalar(
-                small[:, t, 3:4], sums[:, t, 1:2], small[:, t, 0:1], -1.0, ALU.mult, ALU.mult
-            )
-            nc.vector.tensor_scalar(
-                terms[:, t, DEGREE : DEGREE + 1], sums[:, t, 1:2].bitcast(I32), LOG_PER_BIT, small[:, t, 2:3],
+                terms[:, t, DEGREE : DEGREE + 1], sums[:, t, 1:2].bitcast(I32), LOG_PER_BIT, guess[:, t, 0:1],
                 ALU.mult, ALU.subtract,
             )
             nc.vector.tensor_scalar(
-                factors[:, t, 0 : DEGREE + 1], guess[:, t : t + 1].to_broadcast([P, DEGREE + 1]),
-                small[:, t, 3:4], 1.0, ALU.mult, ALU.add,
+                factors[:, t, 0 : DEGREE + 1], guess[:, t, 1:2].to_broadcast([P, DEGREE + 1]),
+                small[:, t, 1:2], 1.0, ALU.mult, ALU.add,
             )
             nc.vector.tensor_tensor_scan(
                 scanned[:, t, :], factors[:, t, :], terms[:, t, :], 0.0, ALU.mult, ALU.add
             )
 
-        nc.vector.scalar_tensor_tensor(weight[:], lam_sb, -1.0, good_sb, ALU.mult, ALU.mult)
+        diff = [keep.tile([P, S], F32, name="diff%d" % t) for t in range(TILES)]
+        reward = [keep.tile([P, S], F32, name="reward%d" % t) for t in range(TILES)]
+        sizes = [keep.tile([P, S], F32, name="sizes%d" % t) for t in range(TILES)]
+        tanh = [keep.tile([P, S], F32, name="tanh%d" % t) for t in range(TILES)]
+        square = [keep.tile([P, S], F32, name="square%d" % t) for t in range(TILES)]
+        result = [keep.tile([P, S], F32, name="result%d" % t) for t in range(TILES)]
+        halves = [slice(0, HALF), slice(HALF, S)]
 
         for t in range(TILES):
-            shift = scanned[:, t, STEPS - 1 : STEPS]
+            softmax_sum(t, 0, h_mx[t])
+            softmax_sum(t, 1, g_mx[t])
+        for t in range(TILES):
+            first_guess(t)
+            second_guess(t)
+            log_ratio(t)
+        for t in range(TILES):
+            for cols in halves:
+                nc.vector.tensor_tensor(diff[t][:, cols], minus[t, 1][:, cols], minus[t, 0][:, cols], ALU.subtract)
+        for t in range(TILES):
             nc.scalar.activation(
-                discard[:], diffs[t][:], ACT.Abs, bias=shift, scale=HALF_BETA, accum_out=sums[:, t, 2:3]
+                sizes[t][:], diff[t][:], ACT.Abs, bias=scanned[:, t, STEPS - 1 : STEPS],
+                scale=HALF_BETA * ZREF_SHARE / S, accum_out=sums[:, t, 2:3],
             )
             nc.vector.tensor_scalar(
-                small[:, t, 1:2], sums[:, t, 2:3], -ZREF_SHARE / S, shift, ALU.mult, ALU.add
+                reward[t][:], diff[t][:], -HALF_BETA, scanned[:, t, STEPS - 2 : STEPS - 1], ALU.mult, ALU.subtract
             )
+        nc.vector.scalar_tensor_tensor(weight[:], lam_sb, -1.0, good_sb, ALU.mult, ALU.mult)
         for t in range(TILES):
-            tanh = keep.tile([P, S], F32, name="tanh%d" % t)
-            square = keep.tile([P, S], F32, name="square%d" % t)
-            result = keep.tile([P, S], F32, name="result%d" % t)
-            nc.scalar.activation(tanh[:], diffs[t][:], ACT.Tanh, bias=small[:, t, 1:2], scale=HALF_BETA)
-            nc.scalar.activation(square[:], tanh[:], ACT.Square, scale=0.5)
-            nc.vector.scalar_tensor_tensor(result[:], square[:], 0.25, weight[:], ALU.subtract, ALU.mult)
-            nc.sync.dma_start(out[t * P : (t + 1) * P, :], result[:])
+            for cols in halves:
+                nc.scalar.activation(tanh[t][:, cols], reward[t][:, cols], ACT.Tanh, bias=sums[:, t, 2:3])
+        for cols in halves:
+            nc.vector.scalar_tensor_tensor(
+                square[0][:, cols], tanh[0][:, cols], 0.25, tanh[0][:, cols], ALU.mult, ALU.mult
+            )
+            nc.scalar.activation(square[1][:, cols], tanh[1][:, cols], ACT.Square, scale=0.5)
+        for t in range(TILES):
+            for cols in halves:
+                nc.vector.scalar_tensor_tensor(
+                    result[t][:, cols], square[t][:, cols], 0.25, weight[:, cols], ALU.subtract, ALU.mult
+                )
+                nc.sync.dma_start(out[t * P : (t + 1) * P, cols], result[t][:, cols])

@@ -1,6 +1,7 @@
 from contextlib import ExitStack
 
 import concourse.mybir as mybir
+from concourse.masks import make_identity
 
 K, T, S, V = 512, 1024, 512, 256
 FLOPS = 2 * 2 * K * V * S
@@ -22,7 +23,7 @@ HALF_BETA = 0.75
 ZREF_SHARE = 0.3
 LOG_PER_BIT = 355.0 / 512.0 / 2.0**23
 DEGREE = 20
-STEPS = DEGREE + 3
+STEPS = DEGREE + 5
 HALF = S // 2
 
 
@@ -33,50 +34,45 @@ def tile_picked_yhkto_grad_p_kernel(tc, x_words, x_scales, hT, gT, good, lam, of
         psum = ctx.enter_context(tc.psum_pool(name="psum", bufs=1))
 
         offsets = keep.tile([P, S // 16], U16, name="offsets")
-        table_scales = keep.tile([P, T], U8, name="table_scales", tag="scales_then_words", align_bytes=64)
+        table_scales = keep.tile([P, T], U8, name="table_scales", align_bytes=64)
         table_words = keep.tile([P, T], I32, name="table_words", align_bytes=64)
-        h_raw = keep.tile([P, PACK, V], F32, name="h_raw", tag="reused")
+        h_raw = [keep.tile([P, PACK, P], F32, name="h_raw%d" % t) for t in range(TILES)]
         g_raw = keep.tile([P, PACK, V], F32, name="g_raw")
+        h_rows = hT.rearrange("(p j) w -> p j w", j=PACK)
 
         nc.vector.memset(table_scales[:].bitcast(I32), 0)
         nc.sync.dma_start(offsets[:], offs)
-        for q in range(4):
-            nc.scalar.dma_start(
+        nc.sync.dma_start(h_raw[0][:], h_rows[:, :, 0:P])
+        for q, queue in enumerate((nc.sync, nc.scalar, nc.sync, nc.scalar)):
+            queue.dma_start(
                 table_scales[32 * q : 32 * q + 4, :].bitcast(I32),
                 x_scales[0, 4 * q : 4 * q + 4, :].bitcast(I32),
             )
         nc.sync.dma_start(table_words[:], x_words[0].rearrange("p n t -> p (n t)").bitcast(I32))
-        nc.sync.dma_start(h_raw[:], hT.rearrange("(p j) w -> p j w", j=PACK))
         nc.sync.dma_start(g_raw[:], gT.rearrange("(p j) w -> p j w", j=PACK))
+        nc.sync.dma_start(h_raw[1][:], h_rows[:, :, P:V])
 
         orders = keep.tile([P, TILES, DEGREE], F32, name="orders")
-        inverse_orders = keep.tile([P, TILES, DEGREE], F32, name="inverse_orders")
         factors = keep.tile([P, TILES, STEPS], F32, name="factors")
         terms = keep.tile([P, TILES, STEPS], F32, name="terms")
         nc.gpsimd.iota(
             orders[:], [[0, TILES], [-1, DEGREE]], base=DEGREE, channel_multiplier=0,
             allow_small_or_imprecise_dtypes=True,
         )
-        nc.vector.reciprocal(inverse_orders[:], orders[:])
-        nc.scalar.activation(terms[:, :, 0:DEGREE], inverse_orders[:], ACT.Copy, scale=-1.0)
-        nc.vector.memset(factors[:, :, DEGREE + 1], HALF_BETA)
-        nc.vector.tensor_scalar(factors[:, :, DEGREE + 2], orders[:, :, DEGREE - 1], ZREF_SHARE / S, None, ALU.mult)
-        nc.vector.memset(terms[:, :, DEGREE + 2], 0.0)
+        nc.vector.reciprocal(terms[:, :, 0:DEGREE], orders[:])
+        nc.vector.memset(terms[:, :, DEGREE + 3 : STEPS], 0.0)
+        nc.vector.memset(factors[:, :, DEGREE + 1 : DEGREE + 3], -1.0)
+        nc.vector.memset(factors[:, :, DEGREE + 3], -HALF_BETA)
+        nc.scalar.activation(factors[:, :, DEGREE + 4], orders[:, :, DEGREE - 1], ACT.Copy, scale=ZREF_SHARE / S)
 
         picked_scales = keep.tile([P, S], U8, name="picked_scales", align_bytes=64)
         nc.vector.tensor_copy(picked_scales[:], table_scales[:].indirect(offsets[:]))
-        picked_words = keep.tile([P, S], U32, name="picked_words", tag="scales_then_words", align_bytes=64)
-        nc.vector.tensor_copy(picked_words[:], table_words[:].bitcast(U32).indirect(offsets[:]))
+        picked_words = keep.tile([P, S], U32, name="picked_words", align_bytes=64)
 
-        def interleave(engine, raw, t, name):
-            grouped = keep.tile([P, P, PACK], BF16, name=name, align_bytes=64)
-            dst = grouped[:].rearrange("p (c i) j -> p c j i", i=4)
-            src = raw[:, :, t * P : (t + 1) * P].rearrange("p j (c i) -> p c j i", i=4)
-            if engine is nc.scalar:
-                nc.scalar.copy(dst, src)
-            else:
-                nc.vector.tensor_copy(dst, src)
-            return grouped
+        halves = [slice(0, HALF), slice(HALF, S)]
+
+        def interleave(copy, raw, grouped):
+            copy(grouped.rearrange("p (c i) j -> p c j i", i=4), raw.rearrange("p j (c i) -> p c j i", i=4))
 
         def quantize(grouped, name):
             codes = keep.tile([P, P], U32, name=name + "_codes", align_bytes=64)
@@ -84,81 +80,97 @@ def tile_picked_yhkto_grad_p_kernel(tc, x_words, x_scales, hT, gT, good, lam, of
             nc.vector.quantize_mx(
                 out=codes[:].bitcast(FP8X4),
                 scales=scales[:],
-                in_=grouped[:].rearrange("p w j -> p (w j)"),
+                in_=grouped.rearrange("p w j -> p (w j)"),
             )
             return codes, scales
 
-        def product(operand, name):
+        def product(operand, name, pieces):
             codes, scales = operand
-            bank = psum.tile([P, S], F32, name=name)
-            nc.tensor.matmul_mx(
-                out=bank[:],
-                lhsT=codes[:].bitcast(FP8X4),
-                lhsT_scale=scales[:],
-                rhs=picked_words[:].bitcast(FP8X4),
-                rhs_scale=picked_scales[:],
-                start=True,
-                stop=True,
-            )
+            bank = psum.tile([P, S], F32, name=name, tag=name)
+            for cols in pieces:
+                nc.tensor.matmul_mx(
+                    out=bank[:, cols],
+                    lhsT=codes[:].bitcast(FP8X4),
+                    lhsT_scale=scales[:],
+                    rhs=picked_words[:, cols].bitcast(FP8X4),
+                    rhs_scale=picked_scales[:, cols],
+                    start=True,
+                    stop=True,
+                )
             return bank
 
-        engines = (nc.vector, nc.scalar)
-        h_bf = [interleave(engines[t], h_raw, t, "h_bf%d" % t) for t in range(TILES)]
-        labels = keep.tile([P, 2, S], F32, name="labels", tag="reused")
-        lam_sb, good_sb = labels[:, 0, :], labels[:, 1, :]
-        nc.sync.dma_start(lam_sb, lam)
-        nc.sync.dma_start(good_sb, good)
-        h_mx = [quantize(h_bf[t], "h%d" % t) for t in range(TILES)]
-        g_bf = [interleave(engines[t], g_raw, t, "g_bf%d" % t) for t in range(TILES)]
-        g_mx = [quantize(g_bf[t], "g%d" % t) for t in range(TILES)]
+        h_bf = [
+            keep.tile([P, P, PACK], BF16, name="h_bf%d" % t, tag="stage%d" % (2 * t), align_bytes=64)
+            for t in range(TILES)
+        ]
+        g_bf = keep.tile([P, V, PACK], BF16, name="g_bf", tag="stage1", align_bytes=64)
+        interleave(nc.scalar.copy, h_raw[0][:], h_bf[0][:])
+        h_mx = [quantize(h_bf[0][:], "h0")]
+        for half, cols in enumerate(halves):
+            nc.vector.tensor_copy(
+                picked_words[:, cols],
+                table_words[:].bitcast(U32).indirect(offsets[:, half * HALF // 16 : (half + 1) * HALF // 16]),
+            )
+        interleave(nc.vector.tensor_copy, g_raw[:, :, 0:P], g_bf[:, 0:P, :])
+        interleave(nc.scalar.copy, g_raw[:, :, P:V], g_bf[:, P:V, :])
+        g_mx = [quantize(g_bf[:, t * P : (t + 1) * P, :], "g%d" % t) for t in range(TILES)]
+        interleave(nc.scalar.copy, h_raw[1][:], h_bf[1][:])
+        h_mx.append(quantize(h_bf[1][:], "h1"))
+        lam_sb = keep.tile([P, PACK], F32, name="lam_sb")
+        good_sb = keep.tile([P, PACK], F32, name="good_sb")
+        minus_lam = keep.tile([P, PACK], F32, name="minus_lam")
+        weight_sb = keep.tile([P, PACK], F32, name="weight_sb")
+        identity = keep.tile([P, P], F32, name="identity")
+        nc.sync.dma_start(lam_sb[:], lam[0].rearrange("(n m) -> n m", m=PACK))
+        nc.sync.dma_start(good_sb[:], good[0].rearrange("(n m) -> n m", m=PACK))
+        make_identity(nc, identity[:])
+        nc.gpsimd.tensor_scalar(minus_lam[:], lam_sb[:], -1.0, 0.0, ALU.mult, ALU.add)
+        nc.gpsimd.tensor_tensor(weight_sb[:], minus_lam[:], good_sb[:], ALU.mult)
 
-        weight = keep.tile([P, S], F32, name="weight")
-        mins = keep.tile([P, TILES, 2], F32, name="mins")
         sums = keep.tile([P, TILES, 3], F32, name="sums")
-        small = keep.tile([P, TILES, 2], F32, name="small")
-        guess = keep.tile([P, TILES, 2], F32, name="guess")
+        small = keep.tile([P, TILES, 3], F32, name="small")
+        guess = keep.tile([P, TILES], F32, name="guess")
         scanned = keep.tile([P, TILES, STEPS], F32, name="scanned")
 
         minus = {}
 
         def softmax_sum(t, side, operand):
-            bank = product(operand, "bank%d%d" % (t, side))
-            minus[t, side] = keep.tile([P, S], F32, name="minus%d%d" % (t, side))
+            first = (t, side) == (0, 0)
+            bank = product(operand, "bank%d%d" % (t, side), halves if first else [slice(0, S)])
+            minus[t, side] = keep.tile(
+                [P, S], F32, name="minus%d%d" % (t, side), tag="stage%d" % (2 * t + side + 1), align_bytes=64
+            )
             exps = keep.tile([P, S], F32, name="exps%d%d" % (t, side))
             nc.vector.tensor_scalar(
-                minus[t, side][:], bank[:], -1.0, None, ALU.mult, ALU.min, accum_out=mins[:, t, side : side + 1]
+                minus[t, side][:], bank[:], -1.0, None, ALU.mult, ALU.min, accum_out=terms[:, t, DEGREE + 1 + side : DEGREE + 2 + side]
             )
             nc.scalar.activation(
-                exps[:], minus[t, side][:], ACT.Exp, bias=mins[:, t, side : side + 1], scale=-1.0,
+                exps[:], minus[t, side][:], ACT.Exp, bias=terms[:, t, DEGREE + 1 + side : DEGREE + 2 + side], scale=-1.0,
                 accum_out=sums[:, t, side : side + 1],
             )
 
         def first_guess(t):
-            nc.scalar.activation(
-                guess[:, t, 0:1], sums[:, t, 0:1].bitcast(U32), ACT.Copy, scale=LOG_PER_BIT
+            nc.vector.tensor_scalar(
+                small[:, t, 2:3], sums[:, t, 0:1].bitcast(I32), LOG_PER_BIT, None, ALU.mult
             )
 
         def second_guess(t):
             nc.scalar.activation(
-                guess[:, t, 1:2], sums[:, t, 1:2].bitcast(U32), ACT.Exp,
-                bias=guess[:, t, 0:1], scale=-LOG_PER_BIT,
+                guess[:, t : t + 1], sums[:, t, 1:2].bitcast(U32), ACT.Exp,
+                bias=small[:, t, 2:3], scale=-LOG_PER_BIT,
             )
 
         def log_ratio(t):
             nc.vector.reciprocal(small[:, t, 0:1], sums[:, t, 0:1])
             nc.vector.tensor_scalar(
-                terms[:, t, DEGREE + 1 : DEGREE + 2], mins[:, t, 0:1], mins[:, t, 1:2], HALF_BETA,
-                ALU.subtract, ALU.mult,
-            )
-            nc.vector.tensor_scalar(
                 small[:, t, 1:2], sums[:, t, 1:2], small[:, t, 0:1], -1.0, ALU.mult, ALU.mult
             )
             nc.vector.tensor_scalar(
-                terms[:, t, DEGREE : DEGREE + 1], sums[:, t, 1:2].bitcast(I32), LOG_PER_BIT, guess[:, t, 0:1],
-                ALU.mult, ALU.subtract,
+                terms[:, t, DEGREE : DEGREE + 1], sums[:, t, 1:2].bitcast(I32), -LOG_PER_BIT, small[:, t, 2:3],
+                ALU.mult, ALU.add,
             )
             nc.vector.tensor_scalar(
-                factors[:, t, 0 : DEGREE + 1], guess[:, t, 1:2].to_broadcast([P, DEGREE + 1]),
+                factors[:, t, 0 : DEGREE + 1], guess[:, t : t + 1].to_broadcast([P, DEGREE + 1]),
                 small[:, t, 1:2], 1.0, ALU.mult, ALU.add,
             )
             nc.vector.tensor_tensor_scan(
@@ -171,38 +183,58 @@ def tile_picked_yhkto_grad_p_kernel(tc, x_words, x_scales, hT, gT, good, lam, of
         tanh = [keep.tile([P, S], F32, name="tanh%d" % t) for t in range(TILES)]
         square = [keep.tile([P, S], F32, name="square%d" % t) for t in range(TILES)]
         result = [keep.tile([P, S], F32, name="result%d" % t) for t in range(TILES)]
-        halves = [slice(0, HALF), slice(HALF, S)]
 
+        softmax_sum(0, 0, h_mx[0])
+        softmax_sum(0, 1, g_mx[0])
+        first_guess(0)
+        second_guess(0)
+        nc.gpsimd.tensor_tensor(diff[0][:], minus[0, 1][:], minus[0, 0][:], ALU.subtract)
+        softmax_sum(1, 0, g_mx[1])
+        softmax_sum(1, 1, h_mx[1])
+        first_guess(1)
+        second_guess(1)
         for t in range(TILES):
-            softmax_sum(t, 0, h_mx[t])
-            softmax_sum(t, 1, g_mx[t])
-        for t in range(TILES):
-            first_guess(t)
-            second_guess(t)
             log_ratio(t)
-        for t in range(TILES):
-            for cols in halves:
-                nc.vector.tensor_tensor(diff[t][:, cols], minus[t, 1][:, cols], minus[t, 0][:, cols], ALU.subtract)
+        for cols in halves:
+            nc.vector.tensor_tensor(diff[1][:, cols], minus[1, 1][:, cols], minus[1, 0][:, cols], ALU.subtract)
         for t in range(TILES):
             nc.scalar.activation(
                 sizes[t][:], diff[t][:], ACT.Abs, bias=scanned[:, t, STEPS - 1 : STEPS],
                 scale=HALF_BETA * ZREF_SHARE / S, accum_out=sums[:, t, 2:3],
             )
+            sign, join = ((-1.0, ALU.subtract), (1.0, ALU.add))[t]
             nc.vector.tensor_scalar(
-                reward[t][:], diff[t][:], -HALF_BETA, scanned[:, t, STEPS - 2 : STEPS - 1], ALU.mult, ALU.subtract
+                reward[t][:], diff[t][:], sign * HALF_BETA, scanned[:, t, STEPS - 2 : STEPS - 1], ALU.mult, join
             )
-        nc.vector.scalar_tensor_tensor(weight[:], lam_sb, -1.0, good_sb, ALU.mult, ALU.mult)
+        weight = psum.tile([P, PACK, P], F32, name="weight", tag="bank10")
+        for m in range(PACK):
+            nc.tensor.transpose(weight[:, m, :], weight_sb[:, m : m + 1].to_broadcast([P, P]), identity[:])
+        weight_by_entry = weight[:].rearrange("p m n -> p n m")
+
+        def squared(t, cols):
+            if t == TILES - 1:
+                nc.scalar.activation(square[t][:, cols], tanh[t][:, cols], ACT.Square, scale=0.5)
+            else:
+                nc.vector.scalar_tensor_tensor(
+                    square[t][:, cols], tanh[t][:, cols], 0.25, tanh[t][:, cols], ALU.mult, ALU.mult
+                )
+
+        def finish(t, cols):
+            nc.vector.scalar_tensor_tensor(
+                result[t][:, cols].rearrange("p (n m) -> p n m", m=PACK),
+                square[t][:, cols].rearrange("p (n m) -> p n m", m=PACK),
+                0.25,
+                weight_by_entry[:, cols.start // PACK : cols.stop // PACK, :],
+                ALU.subtract,
+                ALU.mult,
+            )
+            nc.sync.dma_start(out[t * P : (t + 1) * P, cols], result[t][:, cols])
+
         for t in range(TILES):
             for cols in halves:
                 nc.scalar.activation(tanh[t][:, cols], reward[t][:, cols], ACT.Tanh, bias=sums[:, t, 2:3])
-        for cols in halves:
-            nc.vector.scalar_tensor_tensor(
-                square[0][:, cols], tanh[0][:, cols], 0.25, tanh[0][:, cols], ALU.mult, ALU.mult
-            )
-            nc.scalar.activation(square[1][:, cols], tanh[1][:, cols], ACT.Square, scale=0.5)
         for t in range(TILES):
             for cols in halves:
-                nc.vector.scalar_tensor_tensor(
-                    result[t][:, cols], square[t][:, cols], 0.25, weight[:, cols], ALU.subtract, ALU.mult
-                )
-                nc.sync.dma_start(out[t * P : (t + 1) * P, cols], result[t][:, cols])
+                squared(t, cols)
+            for cols in halves:
+                finish(t, cols)

@@ -5,6 +5,7 @@ from concourse.masks import make_identity
 
 K, T, S, V = 512, 1024, 512, 256
 FLOPS = 2 * 2 * K * V * S
+BYTES = K * T + K // 32 * T + 2 * 4 * K * V + 2 * 4 * S + 2 * 8 * S + 4 * V * S
 
 F32 = mybir.dt.float32
 BF16 = mybir.dt.bfloat16
@@ -18,13 +19,27 @@ ACT = mybir.ActivationFunctionType
 
 P = 128
 PACK = 4
+QUADRANT = 32
+LINE = 4
+PER_COLUMN = 16
+SPREAD = S // P
 TILES = V // P
-HALF_BETA = 0.75
-ZREF_SHARE = 0.3
-LOG_PER_BIT = 355.0 / 512.0 / 2.0**23
-DEGREE = 20
-STEPS = DEGREE + 5
 HALF = S // 2
+
+HALF_BETA = 0.75
+MEAN_SHARE = 0.3 / S
+LOG_PER_BIT = 355.0 / 512.0 / 2.0**23
+
+DEGREE = 20
+GUESS = DEGREE
+FIRST_MAX = DEGREE + 1
+SHIFT = DEGREE + 3
+MEAN_SHIFT = DEGREE + 4
+STEPS = DEGREE + 5
+
+
+def column(index):
+    return slice(index, index + 1)
 
 
 def tile_picked_yhkto_grad_p_kernel(tc, x_words, x_scales, hT, gT, good, lam, offs, out):
@@ -33,7 +48,7 @@ def tile_picked_yhkto_grad_p_kernel(tc, x_words, x_scales, hT, gT, good, lam, of
         keep = ctx.enter_context(tc.tile_pool(name="keep", bufs=1))
         psum = ctx.enter_context(tc.psum_pool(name="psum", bufs=1))
 
-        offsets = keep.tile([P, S // 16], U16, name="offsets")
+        offsets = keep.tile([P, S // PER_COLUMN], U16, name="offsets")
         table_scales = keep.tile([P, T], U8, name="table_scales", align_bytes=64)
         table_words = keep.tile([P, T], I32, name="table_words", align_bytes=64)
         h_raw = [keep.tile([P, PACK, P], F32, name="h_raw%d" % t) for t in range(TILES)]
@@ -45,7 +60,7 @@ def tile_picked_yhkto_grad_p_kernel(tc, x_words, x_scales, hT, gT, good, lam, of
         nc.sync.dma_start(h_raw[0][:], h_rows[:, :, 0:P])
         for q, queue in enumerate((nc.sync, nc.scalar, nc.sync, nc.scalar)):
             queue.dma_start(
-                table_scales[32 * q : 32 * q + 4, :].bitcast(I32),
+                table_scales[QUADRANT * q : QUADRANT * q + 4, :].bitcast(I32),
                 x_scales[0, 4 * q : 4 * q + 4, :].bitcast(I32),
             )
         nc.sync.dma_start(table_words[:], x_words[0].rearrange("p n t -> p (n t)").bitcast(I32))
@@ -60,10 +75,10 @@ def tile_picked_yhkto_grad_p_kernel(tc, x_words, x_scales, hT, gT, good, lam, of
             allow_small_or_imprecise_dtypes=True,
         )
         nc.vector.reciprocal(terms[:, :, 0:DEGREE], orders[:])
-        nc.vector.memset(terms[:, :, DEGREE + 3 : STEPS], 0.0)
-        nc.vector.memset(factors[:, :, DEGREE + 1 : DEGREE + 3], -1.0)
-        nc.vector.memset(factors[:, :, DEGREE + 3], -HALF_BETA)
-        nc.scalar.activation(factors[:, :, DEGREE + 4], orders[:, :, DEGREE - 1], ACT.Copy, scale=ZREF_SHARE / S)
+        nc.vector.memset(terms[:, :, SHIFT:STEPS], 0.0)
+        nc.vector.memset(factors[:, :, FIRST_MAX:SHIFT], -1.0)
+        nc.vector.memset(factors[:, :, SHIFT], -HALF_BETA)
+        nc.scalar.activation(factors[:, :, MEAN_SHIFT], orders[:, :, DEGREE - 1], ACT.Copy, scale=MEAN_SHARE)
 
         picked_scales = keep.tile([P, S], U8, name="picked_scales", align_bytes=64)
         nc.vector.tensor_copy(picked_scales[:], table_scales[:].indirect(offsets[:]))
@@ -72,11 +87,11 @@ def tile_picked_yhkto_grad_p_kernel(tc, x_words, x_scales, hT, gT, good, lam, of
         halves = [slice(0, HALF), slice(HALF, S)]
 
         def interleave(copy, raw, grouped):
-            copy(grouped.rearrange("p (c i) j -> p c j i", i=4), raw.rearrange("p j (c i) -> p c j i", i=4))
+            copy(grouped.rearrange("p (c i) j -> p c j i", i=LINE), raw.rearrange("p j (c i) -> p c j i", i=LINE))
 
         def quantize(grouped, name):
             codes = keep.tile([P, P], U32, name=name + "_codes", align_bytes=64)
-            scales = keep.tile([P, P], U8, name=name + "_scales", align_bytes=64)
+            scales = keep.tile([P, P], U8, name=name + "_scales", tag=name + "_scales", align_bytes=64)
             nc.vector.quantize_mx(
                 out=codes[:].bitcast(FP8X4),
                 scales=scales[:],
@@ -106,76 +121,59 @@ def tile_picked_yhkto_grad_p_kernel(tc, x_words, x_scales, hT, gT, good, lam, of
         g_bf = keep.tile([P, V, PACK], BF16, name="g_bf", tag="stage1", align_bytes=64)
         interleave(nc.scalar.copy, h_raw[0][:], h_bf[0][:])
         h_mx = [quantize(h_bf[0][:], "h0")]
-        for half, cols in enumerate(halves):
-            nc.vector.tensor_copy(
-                picked_words[:, cols],
-                table_words[:].bitcast(U32).indirect(offsets[:, half * HALF // 16 : (half + 1) * HALF // 16]),
-            )
+        for cols in halves:
+            entries = offsets[:, cols.start // PER_COLUMN : cols.stop // PER_COLUMN]
+            nc.vector.tensor_copy(picked_words[:, cols], table_words[:].bitcast(U32).indirect(entries))
         interleave(nc.vector.tensor_copy, g_raw[:, :, 0:P], g_bf[:, 0:P, :])
         interleave(nc.scalar.copy, g_raw[:, :, P:V], g_bf[:, P:V, :])
         g_mx = [quantize(g_bf[:, t * P : (t + 1) * P, :], "g%d" % t) for t in range(TILES)]
         interleave(nc.scalar.copy, h_raw[1][:], h_bf[1][:])
         h_mx.append(quantize(h_bf[1][:], "h1"))
-        lam_sb = keep.tile([P, PACK], F32, name="lam_sb")
-        good_sb = keep.tile([P, PACK], F32, name="good_sb")
-        minus_lam = keep.tile([P, PACK], F32, name="minus_lam")
-        weight_sb = keep.tile([P, PACK], F32, name="weight_sb")
+
+        lam_sb = keep.tile([P, SPREAD], F32, name="lam_sb")
+        good_sb = keep.tile([P, SPREAD], F32, name="good_sb")
         identity = keep.tile([P, P], F32, name="identity")
-        nc.sync.dma_start(lam_sb[:], lam[0].rearrange("(n m) -> n m", m=PACK))
-        nc.sync.dma_start(good_sb[:], good[0].rearrange("(n m) -> n m", m=PACK))
+        nc.sync.dma_start(lam_sb[:], lam[0].rearrange("(n m) -> n m", m=SPREAD))
+        nc.sync.dma_start(good_sb[:], good[0].rearrange("(n m) -> n m", m=SPREAD))
         make_identity(nc, identity[:])
-        nc.gpsimd.tensor_scalar(minus_lam[:], lam_sb[:], -1.0, 0.0, ALU.mult, ALU.add)
-        nc.gpsimd.tensor_tensor(weight_sb[:], minus_lam[:], good_sb[:], ALU.mult)
 
         sums = keep.tile([P, TILES, 3], F32, name="sums")
-        small = keep.tile([P, TILES, 3], F32, name="small")
-        guess = keep.tile([P, TILES], F32, name="guess")
+        ratio = keep.tile([P, TILES, 2], F32, name="ratio")
+        guess = keep.tile([P, TILES, 2], F32, name="guess")
         scanned = keep.tile([P, TILES, STEPS], F32, name="scanned")
 
         minus = {}
 
-        def softmax_sum(t, side, operand):
-            first = (t, side) == (0, 0)
-            bank = product(operand, "bank%d%d" % (t, side), halves if first else [slice(0, S)])
+        def softmax_sum(t, side, operand, pieces):
+            bank = product(operand, "bank%d%d" % (t, side), pieces)
             minus[t, side] = keep.tile(
                 [P, S], F32, name="minus%d%d" % (t, side), tag="stage%d" % (2 * t + side + 1), align_bytes=64
             )
             exps = keep.tile([P, S], F32, name="exps%d%d" % (t, side))
-            nc.vector.tensor_scalar(
-                minus[t, side][:], bank[:], -1.0, None, ALU.mult, ALU.min, accum_out=terms[:, t, DEGREE + 1 + side : DEGREE + 2 + side]
-            )
+            minus_max = terms[:, t, column(FIRST_MAX + side)]
+            nc.vector.tensor_scalar(minus[t, side][:], bank[:], -1.0, None, ALU.mult, ALU.min, accum_out=minus_max)
             nc.scalar.activation(
-                exps[:], minus[t, side][:], ACT.Exp, bias=terms[:, t, DEGREE + 1 + side : DEGREE + 2 + side], scale=-1.0,
-                accum_out=sums[:, t, side : side + 1],
+                exps[:], minus[t, side][:], ACT.Exp, bias=minus_max, scale=-1.0, accum_out=sums[:, t, column(side)]
             )
 
-        def first_guess(t):
-            nc.vector.tensor_scalar(
-                small[:, t, 2:3], sums[:, t, 0:1].bitcast(I32), LOG_PER_BIT, None, ALU.mult
-            )
-
-        def second_guess(t):
+        def exp_of_guess(t):
+            nc.scalar.activation(guess[:, t, 0:1], sums[:, t, 0:1].bitcast(U32), ACT.Copy, scale=LOG_PER_BIT)
             nc.scalar.activation(
-                guess[:, t : t + 1], sums[:, t, 1:2].bitcast(U32), ACT.Exp,
-                bias=small[:, t, 2:3], scale=-LOG_PER_BIT,
+                guess[:, t, 1:2], sums[:, t, 1:2].bitcast(U32), ACT.Exp, bias=guess[:, t, 0:1], scale=-LOG_PER_BIT
             )
 
         def log_ratio(t):
-            nc.vector.reciprocal(small[:, t, 0:1], sums[:, t, 0:1])
+            nc.vector.reciprocal(ratio[:, t, 0:1], sums[:, t, 0:1])
+            nc.vector.tensor_scalar(ratio[:, t, 1:2], sums[:, t, 1:2], ratio[:, t, 0:1], -1.0, ALU.mult, ALU.mult)
             nc.vector.tensor_scalar(
-                small[:, t, 1:2], sums[:, t, 1:2], small[:, t, 0:1], -1.0, ALU.mult, ALU.mult
-            )
-            nc.vector.tensor_scalar(
-                terms[:, t, DEGREE : DEGREE + 1], sums[:, t, 1:2].bitcast(I32), -LOG_PER_BIT, small[:, t, 2:3],
+                terms[:, t, column(GUESS)], sums[:, t, 1:2].bitcast(I32), -LOG_PER_BIT, guess[:, t, 0:1],
                 ALU.mult, ALU.add,
             )
             nc.vector.tensor_scalar(
-                factors[:, t, 0 : DEGREE + 1], guess[:, t : t + 1].to_broadcast([P, DEGREE + 1]),
-                small[:, t, 1:2], 1.0, ALU.mult, ALU.add,
+                factors[:, t, 0:FIRST_MAX], guess[:, t, 1:2].to_broadcast([P, FIRST_MAX]),
+                ratio[:, t, 1:2], 1.0, ALU.mult, ALU.add,
             )
-            nc.vector.tensor_tensor_scan(
-                scanned[:, t, :], factors[:, t, :], terms[:, t, :], 0.0, ALU.mult, ALU.add
-            )
+            nc.vector.tensor_tensor_scan(scanned[:, t, :], factors[:, t, :], terms[:, t, :], 0.0, ALU.mult, ALU.add)
 
         diff = [keep.tile([P, S], F32, name="diff%d" % t) for t in range(TILES)]
         reward = [keep.tile([P, S], F32, name="reward%d" % t) for t in range(TILES)]
@@ -184,47 +182,49 @@ def tile_picked_yhkto_grad_p_kernel(tc, x_words, x_scales, hT, gT, good, lam, of
         square = [keep.tile([P, S], F32, name="square%d" % t) for t in range(TILES)]
         result = [keep.tile([P, S], F32, name="result%d" % t) for t in range(TILES)]
 
-        softmax_sum(0, 0, h_mx[0])
-        softmax_sum(0, 1, g_mx[0])
-        first_guess(0)
-        second_guess(0)
+        whole = [slice(0, S)]
+        softmax_sum(0, 0, h_mx[0], halves)
+        softmax_sum(0, 1, g_mx[0], whole)
+        exp_of_guess(0)
         nc.gpsimd.tensor_tensor(diff[0][:], minus[0, 1][:], minus[0, 0][:], ALU.subtract)
-        softmax_sum(1, 0, g_mx[1])
-        softmax_sum(1, 1, h_mx[1])
-        first_guess(1)
-        second_guess(1)
+        softmax_sum(1, 0, g_mx[1], whole)
+        softmax_sum(1, 1, h_mx[1], whole)
+        exp_of_guess(1)
         for t in range(TILES):
             log_ratio(t)
         for cols in halves:
             nc.vector.tensor_tensor(diff[1][:, cols], minus[1, 1][:, cols], minus[1, 0][:, cols], ALU.subtract)
-        for t in range(TILES):
+
+        for t, (sign, join) in enumerate(((-1.0, ALU.subtract), (1.0, ALU.add))):
             nc.scalar.activation(
-                sizes[t][:], diff[t][:], ACT.Abs, bias=scanned[:, t, STEPS - 1 : STEPS],
-                scale=HALF_BETA * ZREF_SHARE / S, accum_out=sums[:, t, 2:3],
+                sizes[t][:], diff[t][:], ACT.Abs, bias=scanned[:, t, column(MEAN_SHIFT)],
+                scale=HALF_BETA * MEAN_SHARE, accum_out=sums[:, t, 2:3],
             )
-            sign, join = ((-1.0, ALU.subtract), (1.0, ALU.add))[t]
             nc.vector.tensor_scalar(
-                reward[t][:], diff[t][:], sign * HALF_BETA, scanned[:, t, STEPS - 2 : STEPS - 1], ALU.mult, join
+                reward[t][:], diff[t][:], sign * HALF_BETA, scanned[:, t, column(SHIFT)], ALU.mult, join
             )
-        weight = psum.tile([P, PACK, P], F32, name="weight", tag="bank10")
-        for m in range(PACK):
-            nc.tensor.transpose(weight[:, m, :], weight_sb[:, m : m + 1].to_broadcast([P, P]), identity[:])
+
+        weight_sb = keep.tile([P, SPREAD], F32, name="weight_sb", tag="h1_scales", align_bytes=64)
+        nc.vector.scalar_tensor_tensor(weight_sb[:], lam_sb[:], -1.0, good_sb[:], ALU.mult, ALU.mult)
+        weight = psum.tile([P, SPREAD, P], F32, name="weight", tag="bank10")
+        for m in range(SPREAD):
+            nc.tensor.transpose(weight[:, m, :], weight_sb[:, column(m)].to_broadcast([P, P]), identity[:])
         weight_by_entry = weight[:].rearrange("p m n -> p n m")
 
         def squared(t, cols):
-            if t == TILES - 1:
-                nc.scalar.activation(square[t][:, cols], tanh[t][:, cols], ACT.Square, scale=0.5)
-            else:
+            if t == 0:
                 nc.vector.scalar_tensor_tensor(
                     square[t][:, cols], tanh[t][:, cols], 0.25, tanh[t][:, cols], ALU.mult, ALU.mult
                 )
+            else:
+                nc.scalar.activation(square[t][:, cols], tanh[t][:, cols], ACT.Square, scale=0.5)
 
         def finish(t, cols):
             nc.vector.scalar_tensor_tensor(
-                result[t][:, cols].rearrange("p (n m) -> p n m", m=PACK),
-                square[t][:, cols].rearrange("p (n m) -> p n m", m=PACK),
+                result[t][:, cols].rearrange("p (n m) -> p n m", m=SPREAD),
+                square[t][:, cols].rearrange("p (n m) -> p n m", m=SPREAD),
                 0.25,
-                weight_by_entry[:, cols.start // PACK : cols.stop // PACK, :],
+                weight_by_entry[:, cols.start // SPREAD : cols.stop // SPREAD, :],
                 ALU.subtract,
                 ALU.mult,
             )

@@ -52,8 +52,9 @@ def tile_picked_yhkto_grad_p_kernel(tc, x_words, x_scales, hT, gT, good, lam, of
         table_scales = keep.tile([P, T], U8, name="table_scales", align_bytes=64)
         table_words = keep.tile([P, T], I32, name="table_words", align_bytes=64)
         h_raw = [keep.tile([P, PACK, P], F32, name="h_raw%d" % t) for t in range(TILES)]
-        g_raw = keep.tile([P, PACK, V], F32, name="g_raw")
+        g_raw = [keep.tile([P, PACK, P], F32, name="g_raw%d" % t) for t in range(TILES)]
         h_rows = hT.rearrange("(p j) w -> p j w", j=PACK)
+        g_rows = gT.rearrange("(p j) w -> p j w", j=PACK)
 
         nc.vector.memset(table_scales[:].bitcast(I32), 0)
         nc.sync.dma_start(offsets[:], offs)
@@ -64,7 +65,8 @@ def tile_picked_yhkto_grad_p_kernel(tc, x_words, x_scales, hT, gT, good, lam, of
                 x_scales[0, 4 * q : 4 * q + 4, :].bitcast(I32),
             )
         nc.sync.dma_start(table_words[:], x_words[0].rearrange("p n t -> p (n t)").bitcast(I32))
-        nc.sync.dma_start(g_raw[:], gT.rearrange("(p j) w -> p j w", j=PACK))
+        for t in range(TILES):
+            nc.sync.dma_start(g_raw[t][:], g_rows[:, :, t * P : (t + 1) * P])
         nc.sync.dma_start(h_raw[1][:], h_rows[:, :, P:V])
 
         orders = keep.tile([P, TILES, DEGREE], F32, name="orders")
@@ -86,8 +88,10 @@ def tile_picked_yhkto_grad_p_kernel(tc, x_words, x_scales, hT, gT, good, lam, of
 
         halves = [slice(0, HALF), slice(HALF, S)]
 
-        def interleave(copy, raw, grouped):
-            copy(grouped.rearrange("p (c i) j -> p c j i", i=LINE), raw.rearrange("p j (c i) -> p c j i", i=LINE))
+        def interleave(raw, grouped):
+            nc.scalar.copy(
+                grouped.rearrange("p (c i) j -> p c j i", i=LINE), raw.rearrange("p j (c i) -> p c j i", i=LINE)
+            )
 
         def quantize(grouped, name):
             codes = keep.tile([P, P], U32, name=name + "_codes", align_bytes=64)
@@ -119,15 +123,15 @@ def tile_picked_yhkto_grad_p_kernel(tc, x_words, x_scales, hT, gT, good, lam, of
             for t in range(TILES)
         ]
         g_bf = keep.tile([P, V, PACK], BF16, name="g_bf", tag="stage1", align_bytes=64)
-        interleave(nc.scalar.copy, h_raw[0][:], h_bf[0][:])
+        interleave(h_raw[0][:], h_bf[0][:])
         h_mx = [quantize(h_bf[0][:], "h0")]
         for cols in halves:
             entries = offsets[:, cols.start // PER_COLUMN : cols.stop // PER_COLUMN]
             nc.vector.tensor_copy(picked_words[:, cols], table_words[:].bitcast(U32).indirect(entries))
-        interleave(nc.vector.tensor_copy, g_raw[:, :, 0:P], g_bf[:, 0:P, :])
-        interleave(nc.scalar.copy, g_raw[:, :, P:V], g_bf[:, P:V, :])
+        for t in range(TILES):
+            interleave(g_raw[t][:], g_bf[:, t * P : (t + 1) * P, :])
         g_mx = [quantize(g_bf[:, t * P : (t + 1) * P, :], "g%d" % t) for t in range(TILES)]
-        interleave(nc.scalar.copy, h_raw[1][:], h_bf[1][:])
+        interleave(h_raw[1][:], h_bf[1][:])
         h_mx.append(quantize(h_bf[1][:], "h1"))
 
         lam_sb = keep.tile([P, SPREAD], F32, name="lam_sb")

from contextlib import ExitStack

import concourse.mybir as mybir
from concourse.masks import make_identity

K, T, S, V = 512, 1024, 512, 256
FLOPS = 2 * 2 * K * V * S
BYTES = K * T + K // 32 * T + 2 * 4 * K * V + 2 * 4 * S + 2 * 8 * S + 4 * V * S

F32 = mybir.dt.float32
BF16 = mybir.dt.bfloat16
I32 = mybir.dt.int32
U32 = mybir.dt.uint32
U16 = mybir.dt.uint16
U8 = mybir.dt.uint8
FP8X4 = mybir.dt.float8_e4m3fn_x4
ALU = mybir.AluOpType
ACT = mybir.ActivationFunctionType

P = 128
PACK = 4
QUADRANT = 32
LINE = 4
PER_COLUMN = 16
SPREAD = S // P
TILES = V // P
HALF = S // 2

HALF_BETA = 0.75
MEAN_SHARE = 0.3 / S
LOG_PER_BIT = 355.0 / 512.0 / 2.0**23

DEGREE = 20
GUESS = DEGREE
FIRST_MAX = DEGREE + 1
SHIFT = DEGREE + 3
MEAN_SHIFT = DEGREE + 4
STEPS = DEGREE + 5


def column(index):
    return slice(index, index + 1)


def tile_picked_yhkto_grad_p_kernel(tc, x_words, x_scales, hT, gT, good, lam, offs, out):
    nc = tc.nc
    with ExitStack() as ctx:
        keep = ctx.enter_context(tc.tile_pool(name="keep", bufs=1))
        psum = ctx.enter_context(tc.psum_pool(name="psum", bufs=1))

        offsets = keep.tile([P, S // PER_COLUMN], U16, name="offsets")
        table_scales = keep.tile([P, T], U8, name="table_scales", align_bytes=64)
        table_words = keep.tile([P, T], I32, name="table_words", align_bytes=64)
        h_raw = [keep.tile([P, PACK, P], F32, name="h_raw%d" % t) for t in range(TILES)]
        g_raw = [keep.tile([P, PACK, P], F32, name="g_raw%d" % t) for t in range(TILES)]
        h_rows = hT.rearrange("(p j) w -> p j w", j=PACK)
        g_rows = gT.rearrange("(p j) w -> p j w", j=PACK)

        nc.vector.memset(table_scales[:].bitcast(I32), 0)
        nc.sync.dma_start(offsets[:], offs)
        nc.sync.dma_start(h_raw[0][:], h_rows[:, :, 0:P])
        for q, queue in enumerate((nc.sync, nc.scalar, nc.sync, nc.scalar)):
            queue.dma_start(
                table_scales[QUADRANT * q : QUADRANT * q + 4, :].bitcast(I32),
                x_scales[0, 4 * q : 4 * q + 4, :].bitcast(I32),
            )
        nc.sync.dma_start(table_words[:], x_words[0].rearrange("p n t -> p (n t)").bitcast(I32))
        for t in range(TILES):
            nc.sync.dma_start(g_raw[t][:], g_rows[:, :, t * P : (t + 1) * P])
        nc.sync.dma_start(h_raw[1][:], h_rows[:, :, P:V])

        orders = keep.tile([P, TILES, DEGREE], F32, name="orders")
        factors = keep.tile([P, TILES, STEPS], F32, name="factors")
        terms = keep.tile([P, TILES, STEPS], F32, name="terms")
        nc.gpsimd.iota(
            orders[:], [[0, TILES], [-1, DEGREE]], base=DEGREE, channel_multiplier=0,
            allow_small_or_imprecise_dtypes=True,
        )
        nc.vector.reciprocal(terms[:, :, 0:DEGREE], orders[:])
        nc.vector.memset(terms[:, :, SHIFT:STEPS], 0.0)
        nc.vector.memset(factors[:, :, FIRST_MAX:SHIFT], -1.0)
        nc.vector.memset(factors[:, :, SHIFT], -HALF_BETA)
        nc.scalar.activation(factors[:, :, MEAN_SHIFT], orders[:, :, DEGREE - 1], ACT.Copy, scale=MEAN_SHARE)

        picked_scales = keep.tile([P, S], U8, name="picked_scales", align_bytes=64)
        nc.vector.tensor_copy(picked_scales[:], table_scales[:].indirect(offsets[:]))
        picked_words = keep.tile([P, S], U32, name="picked_words", align_bytes=64)

        halves = [slice(0, HALF), slice(HALF, S)]

        def interleave(raw, grouped):
            nc.scalar.copy(
                grouped.rearrange("p (c i) j -> p c j i", i=LINE), raw.rearrange("p j (c i) -> p c j i", i=LINE)
            )

        def quantize(grouped, name):
            codes = keep.tile([P, P], U32, name=name + "_codes", align_bytes=64)
            scales = keep.tile([P, P], U8, name=name + "_scales", tag=name + "_scales", align_bytes=64)
            nc.vector.quantize_mx(
                out=codes[:].bitcast(FP8X4),
                scales=scales[:],
                in_=grouped.rearrange("p w j -> p (w j)"),
            )
            return codes, scales

        def product(operand, name, pieces):
            codes, scales = operand
            bank = psum.tile([P, S], F32, name=name, tag=name)
            for cols in pieces:
                nc.tensor.matmul_mx(
                    out=bank[:, cols],
                    lhsT=codes[:].bitcast(FP8X4),
                    lhsT_scale=scales[:],
                    rhs=picked_words[:, cols].bitcast(FP8X4),
                    rhs_scale=picked_scales[:, cols],
                    start=True,
                    stop=True,
                )
            return bank

        h_bf = [
            keep.tile([P, P, PACK], BF16, name="h_bf%d" % t, tag="stage%d" % (2 * t), align_bytes=64)
            for t in range(TILES)
        ]
        g_bf = keep.tile([P, V, PACK], BF16, name="g_bf", tag="stage1", align_bytes=64)
        interleave(h_raw[0][:], h_bf[0][:])
        h_mx = [quantize(h_bf[0][:], "h0")]
        for cols in halves:
            entries = offsets[:, cols.start // PER_COLUMN : cols.stop // PER_COLUMN]
            nc.vector.tensor_copy(picked_words[:, cols], table_words[:].bitcast(U32).indirect(entries))
        for t in range(TILES):
            interleave(g_raw[t][:], g_bf[:, t * P : (t + 1) * P, :])
        g_mx = [quantize(g_bf[:, t * P : (t + 1) * P, :], "g%d" % t) for t in range(TILES)]
        interleave(h_raw[1][:], h_bf[1][:])
        h_mx.append(quantize(h_bf[1][:], "h1"))

        lam_sb = keep.tile([P, SPREAD], F32, name="lam_sb")
        good_sb = keep.tile([P, SPREAD], F32, name="good_sb")
        identity = keep.tile([P, P], F32, name="identity")
        nc.sync.dma_start(lam_sb[:], lam[0].rearrange("(n m) -> n m", m=SPREAD))
        nc.sync.dma_start(good_sb[:], good[0].rearrange("(n m) -> n m", m=SPREAD))
        make_identity(nc, identity[:])

        sums = keep.tile([P, TILES, 3], F32, name="sums")
        ratio = keep.tile([P, TILES, 2], F32, name="ratio")
        guess = keep.tile([P, TILES, 2], F32, name="guess")
        scanned = keep.tile([P, TILES, STEPS], F32, name="scanned")

        minus = {}

        def softmax_sum(t, side, operand, pieces):
            bank = product(operand, "bank%d%d" % (t, side), pieces)
            minus[t, side] = keep.tile(
                [P, S], F32, name="minus%d%d" % (t, side), tag="stage%d" % (2 * t + side + 1), align_bytes=64
            )
            exps = keep.tile([P, S], F32, name="exps%d%d" % (t, side))
            minus_max = terms[:, t, column(FIRST_MAX + side)]
            nc.vector.tensor_scalar(minus[t, side][:], bank[:], -1.0, None, ALU.mult, ALU.min, accum_out=minus_max)
            nc.scalar.activation(
                exps[:], minus[t, side][:], ACT.Exp, bias=minus_max, scale=-1.0, accum_out=sums[:, t, column(side)]
            )

        def exp_of_guess(t):
            nc.scalar.activation(guess[:, t, 0:1], sums[:, t, 0:1].bitcast(U32), ACT.Copy, scale=LOG_PER_BIT)
            nc.scalar.activation(
                guess[:, t, 1:2], sums[:, t, 1:2].bitcast(U32), ACT.Exp, bias=guess[:, t, 0:1], scale=-LOG_PER_BIT
            )

        def log_ratio(t):
            nc.vector.reciprocal(ratio[:, t, 0:1], sums[:, t, 0:1])
            nc.vector.tensor_scalar(ratio[:, t, 1:2], sums[:, t, 1:2], ratio[:, t, 0:1], -1.0, ALU.mult, ALU.mult)
            nc.vector.tensor_scalar(
                terms[:, t, column(GUESS)], sums[:, t, 1:2].bitcast(I32), -LOG_PER_BIT, guess[:, t, 0:1],
                ALU.mult, ALU.add,
            )
            nc.vector.tensor_scalar(
                factors[:, t, 0:FIRST_MAX], guess[:, t, 1:2].to_broadcast([P, FIRST_MAX]),
                ratio[:, t, 1:2], 1.0, ALU.mult, ALU.add,
            )
            nc.vector.tensor_tensor_scan(scanned[:, t, :], factors[:, t, :], terms[:, t, :], 0.0, ALU.mult, ALU.add)

        diff = [keep.tile([P, S], F32, name="diff%d" % t) for t in range(TILES)]
        reward = [keep.tile([P, S], F32, name="reward%d" % t) for t in range(TILES)]
        sizes = [keep.tile([P, S], F32, name="sizes%d" % t) for t in range(TILES)]
        tanh = [keep.tile([P, S], F32, name="tanh%d" % t) for t in range(TILES)]
        square = [keep.tile([P, S], F32, name="square%d" % t) for t in range(TILES)]
        result = [keep.tile([P, S], F32, name="result%d" % t) for t in range(TILES)]

        whole = [slice(0, S)]
        softmax_sum(0, 0, h_mx[0], halves)
        softmax_sum(0, 1, g_mx[0], whole)
        exp_of_guess(0)
        nc.gpsimd.tensor_tensor(diff[0][:], minus[0, 1][:], minus[0, 0][:], ALU.subtract)
        softmax_sum(1, 0, g_mx[1], whole)
        softmax_sum(1, 1, h_mx[1], whole)
        exp_of_guess(1)
        for t in range(TILES):
            log_ratio(t)
        for cols in halves:
            nc.vector.tensor_tensor(diff[1][:, cols], minus[1, 1][:, cols], minus[1, 0][:, cols], ALU.subtract)

        for t, (sign, join) in enumerate(((-1.0, ALU.subtract), (1.0, ALU.add))):
            nc.scalar.activation(
                sizes[t][:], diff[t][:], ACT.Abs, bias=scanned[:, t, column(MEAN_SHIFT)],
                scale=HALF_BETA * MEAN_SHARE, accum_out=sums[:, t, 2:3],
            )
            nc.vector.tensor_scalar(
                reward[t][:], diff[t][:], sign * HALF_BETA, scanned[:, t, column(SHIFT)], ALU.mult, join
            )

        weight_sb = keep.tile([P, SPREAD], F32, name="weight_sb", tag="h1_scales", align_bytes=64)
        nc.vector.scalar_tensor_tensor(weight_sb[:], lam_sb[:], -1.0, good_sb[:], ALU.mult, ALU.mult)
        weight = psum.tile([P, SPREAD, P], F32, name="weight", tag="bank10")
        for m in range(SPREAD):
            nc.tensor.transpose(weight[:, m, :], weight_sb[:, column(m)].to_broadcast([P, P]), identity[:])
        weight_by_entry = weight[:].rearrange("p m n -> p n m")

        def squared(t, cols):
            if t == 0:
                nc.vector.scalar_tensor_tensor(
                    square[t][:, cols], tanh[t][:, cols], 0.25, tanh[t][:, cols], ALU.mult, ALU.mult
                )
            else:
                nc.scalar.activation(square[t][:, cols], tanh[t][:, cols], ACT.Square, scale=0.5)

        def finish(t, cols):
            nc.vector.scalar_tensor_tensor(
                result[t][:, cols].rearrange("p (n m) -> p n m", m=SPREAD),
                square[t][:, cols].rearrange("p (n m) -> p n m", m=SPREAD),
                0.25,
                weight_by_entry[:, cols.start // SPREAD : cols.stop // SPREAD, :],
                ALU.subtract,
                ALU.mult,
            )
            nc.sync.dma_start(out[t * P : (t + 1) * P, cols], result[t][:, cols])

        for t in range(TILES):
            for cols in halves:
                nc.scalar.activation(tanh[t][:, cols], reward[t][:, cols], ACT.Tanh, bias=sums[:, t, 2:3])
        for t in range(TILES):
            for cols in halves:
                squared(t, cols)
            for cols in halves:
                finish(t, cols)
